import numpy as np
import ml_dtypes


def mxq(x, axis, fmt="e4m3"):
    dtype, down = {"e4m3": (ml_dtypes.float8_e4m3fn, 7), "e5m2": (ml_dtypes.float8_e5m2, 14)}[fmt]
    v = np.moveaxis(np.asarray(x, np.float32).astype(ml_dtypes.bfloat16).astype(np.float64), axis, -1)
    blocks = v.reshape(v.shape[:-1] + (-1, 32))
    amax = np.abs(blocks).max(-1, keepdims=True)
    byte = np.maximum(np.where(amax > 0, np.frexp(amax)[1] - 1 + 127, 0) - down, 1)
    scale = np.exp2(byte - 127.0)
    codes = (blocks / scale).astype(np.float32).astype(dtype).astype(np.float64)
    return np.moveaxis((codes * scale).reshape(v.shape), -1, axis)


WIDE = False


def mx_kscale(k):
    if not WIDE:
        return np.ones(k)
    levels = np.array([10, -10, 5, -5, 0])
    if k % 512:
        return np.exp2(np.random.permutation(np.resize(levels, k // 32))).repeat(32)
    a = np.empty((k // 512, 16))
    for p in range(k // 512):
        a[p, :8] = np.random.permutation(np.resize(levels, 8))
        for g in range(8):
            far = levels[np.abs(levels - a[p, g]) >= 10]
            a[p, g + 8] = far[np.random.randint(len(far))]
    return np.exp2(a.ravel()).repeat(32)


def f64(x):
    return np.asarray(x).astype(np.float64)


def striped(idx):
    return np.tile(idx.reshape(-1, 16).T, (8, 1)).astype(np.uint16)


def unstriped(offs):
    return offs[:16].T.reshape(-1).astype(np.int64)


def striped8(idx):
    return np.concatenate([x.reshape(-1, 16).T for x in idx]).astype(np.uint16)


def runs(offs, k):
    lists = np.stack([offs[16 * r : 16 * r + 16].T.reshape(-1) for r in range(8)]).astype(np.int64)
    return lists[np.arange(k) % 512 // 64]


def pack_weight(w):
    k, n = w.shape
    w = f64(np.asarray(w, np.float32).astype(ml_dtypes.bfloat16)).reshape(k // 32, 32, n)
    amax = np.abs(w).max(1)
    byte = np.clip(np.where(amax > 0, np.frexp(amax)[1] - 1 + 127 - 7, 1), 1, 254)
    scaled = (w * np.exp2(127.0 - byte)[:, None, :]).reshape(k, n).astype(np.float32)
    words = np.ascontiguousarray(scaled.reshape(k // 512, 128, 4, n).transpose(0, 1, 3, 2)).astype(ml_dtypes.float8_e4m3fn).view(np.uint8)
    return words, np.ascontiguousarray(byte.astype(np.uint8).reshape(k // 512, 16, n))


def unpack_weight(words, scales):
    g, p, n, _ = words.shape
    vals = np.ascontiguousarray(words).view(ml_dtypes.float8_e4m3fn).astype(np.float64) * np.repeat(np.exp2(scales.astype(np.float64) - 127.0), 8, axis=1)[..., None]
    return vals.transpose(0, 1, 3, 2).reshape(g * 512, n)


K, T, S, N, H, W = 512, 2048, 512, 512, 512, 2048


def setup_inputs():
    n = np.random.standard_normal
    s = mx_kscale(K)[:, None]
    u = mx_kscale(H)
    packed_xT = pack_weight(n((K, T)) * s)
    return {
        "x_words": packed_xT[0],
        "x_scales": packed_xT[1],
        "w1": (n((K, H)) / np.sqrt(K) / s).astype(np.float32),
        "gn": (np.random.uniform(0.5, 1.5, (H, 1)) * u[:, None]).astype(np.float32),
        "w2": (n((H, N)) / np.sqrt(2 * H) / u[:, None]).astype(np.float32),
        "w3": (n((K, N)) / np.sqrt(2 * K) / s).astype(np.float32),
        "offs": striped(np.random.permutation(T)[:S]),
        "n1": striped(np.random.randint(0, S, W)),
        "hz": striped8(np.random.randint(0, T, (8, S))),
        "n2": striped8(np.stack([np.random.permutation(S) for _ in range(8)])),
        "n3": striped8(np.stack([np.random.permutation(S) for _ in range(8)])),
    }


def reference(x_words, x_scales, w1, gn, w2, w3, offs, n1, hz, n2, n3):
    xq = unpack_weight(x_words, x_scales)[:, unstriped(offs)]
    y = mxq(f64(w1), 0, "e4m3").T @ xq
    ex = np.exp(0.5 * y)
    mb = ex[:, unstriped(n1)]
    ms = mb.reshape(H, S, 4).sum(axis=2)
    z = f64(gn) * ((4.0 * ex) / (ms + 0.5))
    x_hz = unpack_weight(x_words, x_scales)[np.arange(K)[:, None], runs(hz, K)]
    h = mxq(f64(w2), 0, "e4m3").T @ mxq(z, 0, "e4m3") + mxq(f64(w3), 0, "e4m3").T @ x_hz
    return h[np.arange(N)[:, None], runs(n2, N)] - (h[np.arange(N)[:, None], runs(n3, N)])

@@ -1,0 +1,248 @@
+from contextlib import ExitStack
+
+import concourse.mybir as mybir
+from concourse.masks import make_identity
+
+K, T, S, N, H, W = 512, 2048, 512, 512, 512, 2048
+FLOPS = 3 * 2 * 512 * 512 * 512
+
+F32 = mybir.dt.float32
+BF16 = mybir.dt.bfloat16
+I32 = mybir.dt.int32
+U32 = mybir.dt.uint32
+U16 = mybir.dt.uint16
+U8 = mybir.dt.uint8
+FP8X4 = mybir.dt.float8_e4m3fn_x4
+ACT = mybir.ActivationFunctionType
+ALU = mybir.AluOpType
+
+P = 128
+PACK = 4
+BLOCK = 128
+SPARE = 192
+ON_VECTOR = {(b, t) for b in range(4) for t in (0, 2)}
+PAIRED = set()
+
+
+def tile_picked_mixhgsharegap_none_p_kernel(tc, x_words, x_scales, w1, gn, w2, w3, offs, n1, hz, n2, n3, out):
+    nc = tc.nc
+    blocks = S // BLOCK
+    with ExitStack() as ctx:
+        keep = ctx.enter_context(tc.tile_pool(name="keep", bufs=1))
+        psum = ctx.enter_context(tc.psum_pool(name="psum", bufs=1))
+
+        def load_list(src, name):
+            lst = keep.tile(list(src.shape), U16, name=name)
+            nc.sync.dma_start(lst[:], src)
+            return lst
+
+        def load_weight(w, name):
+            raw = keep.tile([P, PACK, 512], F32, name=name)
+            nc.sync.dma_start(raw[:], w.rearrange("(p j) c -> p j c", j=PACK))
+            return raw
+
+        def round_weight(raw, name, on_scalar=0):
+            grouped = keep.tile([P, PACK, P, PACK], BF16, name=name, align_bytes=64)
+            dst = grouped[:].rearrange("p t m j -> p m j t")
+            src = raw[:].rearrange("p j (m t) -> p m j t", t=PACK)
+            if on_scalar:
+                nc.scalar.copy(dst[:, :on_scalar], src[:, :on_scalar])
+            nc.vector.tensor_copy(dst[:, on_scalar:], src[:, on_scalar:])
+            return grouped
+
+        def quantise_weight(grouped, name):
+            codes = keep.tile([P, 512], U32, name=name + "_codes", align_bytes=64)
+            scales = keep.tile([P, 512], U8, name=name + "_scales", align_bytes=64)
+            nc.vector.quantize_mx(
+                out=codes[:].bitcast(FP8X4), scales=scales[:], in_=grouped[:].rearrange("p t m j -> p (t m j)")
+            )
+            return codes, scales
+
+        table_scales = keep.tile([P, T], U8, name="table_scales")
+        nc.vector.memset(table_scales[:].bitcast(I32), 0)
+        offs_sb = load_list(offs, "offs_sb")
+        n1_sb = load_list(n1, "n1_sb")
+        gain = keep.tile([P, PACK], F32, name="gain")
+        nc.sync.dma_start(gain[:], gn.rearrange("(p t) o -> p (t o)", t=PACK))
+        hz_sb = load_list(hz, "hz_sb")
+        n3_sb = load_list(n3, "n3_sb")
+        n2_sb = load_list(n2, "n2_sb")
+        w1_rows = w1.rearrange("(p j) c -> p j c", j=PACK)
+        w1_raw = [keep.tile([P, PACK, 256], F32, name="w1_raw%d" % u) for u in range(2)]
+        for u in range(2):
+            nc.sync.dma_start(w1_raw[u][:], w1_rows[:, :, 256 * u : 256 * (u + 1)])
+        for r in range(2):
+            nc.sync.dma_start(table_scales[r:P:16, :].bitcast(I32), x_scales[0, r:16:2, :].bitcast(I32))
+            nc.sync.dma_start(table_scales[2 + r : P : 32, :].bitcast(I32), x_scales[0, 2 + r : 16 : 4, :].bitcast(I32))
+        table_words = keep.tile([P, T], U32, name="table_words")
+        nc.sync.dma_start(table_words[:].bitcast(I32), x_words[0].rearrange("p c r -> p (c r)").bitcast(I32))
+        w3_raw = load_weight(w3, "w3_raw")
+        w2_raw = load_weight(w2, "w2_raw")
+
+        ex = [keep.tile([P, S + SPARE], F32, name="ex%d" % t) for t in range(PACK)]
+        for t in range(PACK):
+            nc.gpsimd.memset(ex[t][:, S:], 0.0)
+        hz_scales = keep.tile([P, S], U8, name="hz_scales", align_bytes=64)
+        nc.gpsimd.memset(hz_scales[:], 0)
+
+        ident = keep.tile([P, P], F32, name="ident")
+        make_identity(nc, ident[:])
+
+        x_sc = keep.tile([P, S], U8, name="x_sc", align_bytes=64)
+        nc.vector.tensor_copy(x_sc[:], table_scales[:].indirect(offs_sb[:]))
+        w1_bf = keep.tile([P, PACK, P, PACK], BF16, name="w1_bf", align_bytes=64)
+        for u in range(2):
+            nc.scalar.copy(
+                w1_bf[:, :, 64 * u : 64 * (u + 1), :].rearrange("p t m j -> p m j t"),
+                w1_raw[u][:].rearrange("p j (m t) -> p m j t", t=PACK),
+            )
+        w1_codes, w1_scales = quantise_weight(w1_bf, "w1")
+        x_codes = keep.tile([P, S], U32, name="x_codes", align_bytes=64)
+        nc.vector.tensor_copy(x_codes[:], table_words[:].indirect(offs_sb[:]))
+        hz_sc_raw = keep.tile([P, S], U8, name="hz_sc_raw")
+        nc.vector.tensor_copy(hz_sc_raw[:], table_scales[:].indirect(hz_sb[:]))
+        for dst, src in ((0, 0), (1, 1), (2, 16), (3, 17)):
+            nc.sync.dma_start(hz_scales[dst:P:32, :].bitcast(I32), hz_sc_raw[src:P:32, :].bitcast(I32))
+
+        for t in range(PACK):
+            y = psum.tile([P, S], F32, name="y%d" % t, tag="bank%d" % t)
+            cols = slice(P * t, P * (t + 1))
+            nc.tensor.matmul_mx(
+                out=y[:], lhsT=w1_codes[:, cols].bitcast(FP8X4), lhsT_scale=w1_scales[:, cols],
+                rhs=x_codes[:].bitcast(FP8X4), rhs_scale=x_sc[:], start=True, stop=True,
+            )
+            nc.scalar.activation(ex[t][:, :S], y[:], ACT.Exp, scale=0.5)
+
+        hz_codes = keep.tile([P, S], U32, name="hz_codes", align_bytes=64)
+        nc.vector.tensor_copy(hz_codes[:], table_words[:].indirect(hz_sb[:]))
+
+        z_codes = keep.tile([P, S], U32, name="z_codes", align_bytes=64)
+        z_scales = keep.tile([P, S], U8, name="z_scales", align_bytes=64)
+        h_acc = {}
+        gained = keep.tile([P, PACK, S], F32, name="gained")
+        h = [keep.tile([P, S], F32, name="h%d" % t) for t in range(PACK)]
+        totals, shares = {}, {}
+        last = blocks - 1
+
+        def fetch(b, tiles, bank):
+            entries = n1_sb[:, 32 * b : 32 * (b + 1)]
+            total = psum.tile([P, len(tiles), P], F32, name="total%d_%d" % (b, tiles[0]), tag="bank%d" % bank)
+            for n, t in enumerate(tiles):
+                members = keep.tile([P, 4 * BLOCK], F32, name="members%d_%d" % (b, t), tag="members", bufs=6)
+                if (b, t) in ON_VECTOR:
+                    nc.vector.tensor_copy(members[:].bitcast(U32).rearrange("p (u j) -> p j u", u=4), ex[t][:].bitcast(U32).indirect(entries))
+                    parts = [members[:, BLOCK * u : BLOCK * (u + 1)] for u in range(4)]
+                else:
+                    nc.scalar.activation(members[:], ex[t][:].indirect(entries), ACT.Copy)
+                    parts = [members[:, u::4] for u in range(4)]
+                if (b, t) in PAIRED:
+                    pairs = keep.tile([P, 2 * BLOCK], F32, name="pairs%d_%d" % (b, t))
+                    nc.vector.tensor_tensor(pairs[:].rearrange("p (u j) -> p j u", u=2), members[:, 0::2].rearrange("p (j u) -> p j u", u=2), members[:, 1::2].rearrange("p (j u) -> p j u", u=2), ALU.add)
+                    parts = [pairs[:, BLOCK * u : BLOCK * (u + 1)] for u in range(2)]
+                for u, part in enumerate(parts):
+                    nc.tensor.matmul(
+                        total[:, n, :], lhsT=part, rhs=ident[:], is_transpose=True, start=(u == 0), stop=(u == len(parts) - 1)
+                    )
+            totals[b, tiles[0]] = total
+
+        def invert(b, tiles):
+            width = len(tiles) * P
+            root = keep.tile([P, width], F32, name="root%d_%d" % (b, tiles[0]))
+            nc.scalar.activation(root[:], totals[b, tiles[0]][:].rearrange("p t m -> p (t m)"), ACT.Abs_reciprocal_sqrt, scale=0.25, bias=0.125)
+            inverse = keep.tile([P, width], F32, name="inverse%d_%d" % (b, tiles[0]))
+            nc.scalar.activation(inverse[:], root[:], ACT.Square)
+            if b not in shares:
+                shares[b] = psum.tile([P, PACK, BLOCK], F32, name="share%d" % b, tag="bank%d" % (1 + b % 3))
+            for n, t in enumerate(tiles):
+                nc.tensor.transpose(shares[b][:, t, :], inverse[:, P * n : P * (n + 1)], ident[:])
+
+        def product(t, acc, codes, scales, rhs_codes, rhs_scales, cols, start, stop):
+            rows = slice(P * t, P * (t + 1))
+            nc.tensor.matmul_mx(
+                out=acc, lhsT=codes[:, rows].bitcast(FP8X4), lhsT_scale=scales[:, rows],
+                rhs=rhs_codes[:, cols].bitcast(FP8X4), rhs_scale=rhs_scales[:, cols], start=start, stop=stop,
+            )
+
+        def open_bank(t):
+            h_acc[t] = psum.tile([P, 3 * BLOCK], F32, name="h_acc%d" % t, tag="bank%d" % (4, 5, 6, 2)[t])
+            product(t, h_acc[t][:, : 2 * BLOCK], w3_codes, w3_scales, hz_codes, hz_scales, slice(0, 2 * BLOCK), True, False)
+            product(t, h_acc[t][:, 2 * BLOCK :], w3_codes, w3_scales, hz_codes, hz_scales, slice(2 * BLOCK, 3 * BLOCK), False, False)
+
+        woven = keep.tile([P, S, PACK], BF16, name="z_woven", align_bytes=64)
+
+        def weave(b):
+            cols = slice(BLOCK * b, BLOCK * (b + 1))
+            nc.vector.tensor_tensor(
+                woven[:, cols, :], shares[b][:].rearrange("p t j -> p j t"), gained[:, :, cols].rearrange("p t j -> p j t"), ALU.mult
+            )
+
+        def quantise_z(cols):
+            nc.vector.quantize_mx(
+                out=z_codes[:, cols].bitcast(FP8X4), scales=z_scales[:, cols], in_=woven[:, cols, :].rearrange("p j t -> p (j t)")
+            )
+
+        every = (0, 1, 2, 3)
+        first_two, third, late = slice(0, 2 * BLOCK), slice(2 * BLOCK, 3 * BLOCK), slice(last * BLOCK, S)
+        fetch(0, every, 4)
+        fetch(1, every, 5)
+        w3_bf = round_weight(w3_raw, "w3_bf")
+        for t in range(PACK):
+            nc.vector.tensor_scalar(gained[:, t, :], ex[t][:, :S], gain[:, t : t + 1], None, ALU.mult)
+        w3_codes, w3_scales = quantise_weight(w3_bf, "w3")
+        invert(0, every)
+        fetch(2, every, 6)
+        open_bank(0)
+        w2_bf = round_weight(w2_raw, "w2_bf")
+        invert(1, every)
+        open_bank(1)
+        w2_codes, w2_scales = quantise_weight(w2_bf, "w2")
+        weave(0)
+        invert(2, every)
+        fetch(3, (0, 1), 7)
+        weave(1)
+        open_bank(2)
+        fetch(3, (2, 3), 0)
+        open_bank(3)
+        quantise_z(first_two)
+        for t in range(PACK):
+            product(t, h_acc[t][:, first_two], w2_codes, w2_scales, z_codes, z_scales, first_two, False, False)
+        weave(2)
+        invert(3, (0, 1))
+        invert(3, (2, 3))
+        quantise_z(third)
+        for t in range(PACK):
+            product(t, h_acc[t][:, third], w2_codes, w2_scales, z_codes, z_scales, third, False, True)
+        weave(3)
+        quantise_z(late)
+        for t in range(PACK):
+            nc.scalar.copy(h[t][:, : 3 * BLOCK], h_acc[t][:])
+        for u in range(2):
+            h_late = psum.tile([P, 2, BLOCK], F32, name="h_late%d" % u, tag="bank%d" % (7, 0)[u])
+            for n in range(2):
+                product(2 * u + n, h_late[:, n, :], w3_codes, w3_scales, hz_codes, hz_scales, late, n == 0, False)
+            for n in range(2):
+                product(2 * u + n, h_late[:, n, :], w2_codes, w2_scales, z_codes, z_scales, late, False, n == 1)
+            for n in range(2):
+                if u == 0:
+                    nc.vector.tensor_copy(h[2 * u + n][:, late], h_late[:, n, :])
+                else:
+                    nc.scalar.copy(h[2 * u + n][:, late], h_late[:, n, :])
+
+        out_rows = out.rearrange("(p t) j -> p t j", t=PACK)
+        half = S // 2
+        units = [(t, u) for t in range(PACK) for u in range(2)]
+        for n, (t, u) in enumerate(units):
+            entries = slice(16 * u, 16 * (u + 1))
+            second = keep.tile([P, half], F32, name="second%d" % n)
+            nc.scalar.activation(second[:], h[t][:].indirect(n3_sb[:, entries]), ACT.Copy)
+            gap = keep.tile([P, half], F32, name="gap%d" % n)
+            if n == 0 or n >= 6:
+                first = keep.tile([P, half], F32, name="first%d" % n)
+                if n == 0:
+                    nc.vector.tensor_copy(first[:], h[t][:].indirect(n2_sb[:, entries]))
+                else:
+                    nc.scalar.activation(first[:], h[t][:].indirect(n2_sb[:, entries]), ACT.Copy)
+                nc.vector.tensor_tensor(gap[:], first[:], second[:], ALU.subtract)
+            else:
+                nc.vector.tensor_tensor(gap[:], h[t][:].indirect(n2_sb[:, entries]), second[:], ALU.subtract)
+            nc.sync.dma_start(out_rows[:, t, half * u : half * (u + 1)], gap[:])

@@ -43,8 +43,8 @@ def tile_picked_mixhgsharegap_none_p_kernel(tc, x_words, x_scales, w1, gn, w2, w
 
         def round_weight(raw, name, on_scalar=0):
             grouped = keep.tile([P, PACK, P, PACK], BF16, name=name, align_bytes=64)
-            dst = grouped[:].rearrange("p t m j -> p m j t")
-            src = raw[:].rearrange("p j (m t) -> p m j t", t=PACK)
+            dst = grouped[:].rearrange("p t m j -> p m t j")
+            src = raw[:].rearrange("p j (m t) -> p m t j", t=PACK)
             if on_scalar:
                 nc.scalar.copy(dst[:, :on_scalar], src[:, :on_scalar])
             nc.vector.tensor_copy(dst[:, on_scalar:], src[:, on_scalar:])
@@ -58,26 +58,33 @@ def tile_picked_mixhgsharegap_none_p_kernel(tc, x_words, x_scales, w1, gn, w2, w
             )
             return codes, scales
 
-        table_scales = keep.tile([P, T], U8, name="table_scales")
-        nc.vector.memset(table_scales[:].bitcast(I32), 0)
+        staged_scales = keep.tile([P, T], U8, name="staged_scales")
+        for r in range(4):
+            nc.sync.dma_start(staged_scales[r:P:32, :].bitcast(I32), x_scales[0, r:16:4, :].bitcast(I32))
         offs_sb = load_list(offs, "offs_sb")
-        n1_sb = load_list(n1, "n1_sb")
-        gain = keep.tile([P, PACK], F32, name="gain")
-        nc.sync.dma_start(gain[:], gn.rearrange("(p t) o -> p (t o)", t=PACK))
-        hz_sb = load_list(hz, "hz_sb")
-        n3_sb = load_list(n3, "n3_sb")
-        n2_sb = load_list(n2, "n2_sb")
         w1_rows = w1.rearrange("(p j) c -> p j c", j=PACK)
         w1_raw = [keep.tile([P, PACK, 256], F32, name="w1_raw%d" % u) for u in range(2)]
         for u in range(2):
             nc.sync.dma_start(w1_raw[u][:], w1_rows[:, :, 256 * u : 256 * (u + 1)])
+        hz_sb = load_list(hz, "hz_sb")
+        table_scales = keep.tile([P, T], U8, name="table_scales")
+        nc.vector.memset(table_scales[:].bitcast(I32), 0)
+        for q in range(4):
+            rows = slice(32 * q, 32 * q + 4)
+            nc.vector.tensor_copy(table_scales[rows, :].bitcast(I32), staged_scales[rows, :].bitcast(I32))
+        run_scales = keep.tile([P, T], U8, name="run_scales")
+        nc.vector.memset(run_scales[:].bitcast(I32), 0)
         for r in range(2):
-            nc.sync.dma_start(table_scales[r:P:16, :].bitcast(I32), x_scales[0, r:16:2, :].bitcast(I32))
-            nc.sync.dma_start(table_scales[2 + r : P : 32, :].bitcast(I32), x_scales[0, 2 + r : 16 : 4, :].bitcast(I32))
+            nc.sync.dma_start(run_scales[r:P:16, :].bitcast(I32), x_scales[0, r:16:2, :].bitcast(I32))
         table_words = keep.tile([P, T], U32, name="table_words")
         nc.sync.dma_start(table_words[:].bitcast(I32), x_words[0].rearrange("p c r -> p (c r)").bitcast(I32))
+        n1_sb = load_list(n1, "n1_sb")
         w3_raw = load_weight(w3, "w3_raw")
+        gain = keep.tile([P, PACK], F32, name="gain")
+        nc.sync.dma_start(gain[:], gn.rearrange("(p t) o -> p (t o)", t=PACK))
         w2_raw = load_weight(w2, "w2_raw")
+        n3_sb = load_list(n3, "n3_sb")
+        n2_sb = load_list(n2, "n2_sb")
 
         ex = [keep.tile([P, S + SPARE], F32, name="ex%d" % t) for t in range(PACK)]
         for t in range(PACK):
@@ -93,14 +100,14 @@ def tile_picked_mixhgsharegap_none_p_kernel(tc, x_words, x_scales, w1, gn, w2, w
         w1_bf = keep.tile([P, PACK, P, PACK], BF16, name="w1_bf", align_bytes=64)
         for u in range(2):
             nc.scalar.copy(
-                w1_bf[:, :, 64 * u : 64 * (u + 1), :].rearrange("p t m j -> p m j t"),
-                w1_raw[u][:].rearrange("p j (m t) -> p m j t", t=PACK),
+                w1_bf[:, :, 64 * u : 64 * (u + 1), :].rearrange("p t m j -> p m t j"),
+                w1_raw[u][:].rearrange("p j (m t) -> p m t j", t=PACK),
             )
         w1_codes, w1_scales = quantise_weight(w1_bf, "w1")
         x_codes = keep.tile([P, S], U32, name="x_codes", align_bytes=64)
         nc.vector.tensor_copy(x_codes[:], table_words[:].indirect(offs_sb[:]))
         hz_sc_raw = keep.tile([P, S], U8, name="hz_sc_raw")
-        nc.vector.tensor_copy(hz_sc_raw[:], table_scales[:].indirect(hz_sb[:]))
+        nc.vector.tensor_copy(hz_sc_raw[:], run_scales[:].indirect(hz_sb[:]))
         for dst, src in ((0, 0), (1, 1), (2, 16), (3, 17)):
             nc.sync.dma_start(hz_scales[dst:P:32, :].bitcast(I32), hz_sc_raw[src:P:32, :].bitcast(I32))
 
@@ -130,8 +137,8 @@ def tile_picked_mixhgsharegap_none_p_kernel(tc, x_words, x_scales, w1, gn, w2, w
             for n, t in enumerate(tiles):
                 members = keep.tile([P, 4 * BLOCK], F32, name="members%d_%d" % (b, t), tag="members", bufs=6)
                 if (b, t) in ON_VECTOR:
-                    nc.vector.tensor_copy(members[:].bitcast(U32).rearrange("p (u j) -> p j u", u=4), ex[t][:].bitcast(U32).indirect(entries))
-                    parts = [members[:, BLOCK * u : BLOCK * (u + 1)] for u in range(4)]
+                    nc.vector.tensor_copy(members[:].bitcast(U32).rearrange("p (u j e) -> p j u e", u=2, e=2), ex[t][:].bitcast(U32).indirect(entries))
+                    parts = [members[:, 2 * BLOCK * u + e : 2 * BLOCK * (u + 1) : 2] for u in range(2) for e in range(2)]
                 else:
                     nc.scalar.activation(members[:], ex[t][:].indirect(entries), ACT.Copy)
                     parts = [members[:, u::4] for u in range(4)]

@@ -20,7 +20,7 @@ P = 128
 PACK = 4
 BLOCK = 128
 SPARE = 192
-ON_VECTOR = {(b, t) for b in range(4) for t in (0, 2)}
+ON_VECTOR = {(b, t) for b, n in enumerate((2, 2, 2, 3)) for t in range(4 - n, 4)}
 PAIRED = set()
 
 
@@ -135,7 +135,7 @@ def tile_picked_mixhgsharegap_none_p_kernel(tc, x_words, x_scales, w1, gn, w2, w
             entries = n1_sb[:, 32 * b : 32 * (b + 1)]
             total = psum.tile([P, len(tiles), P], F32, name="total%d_%d" % (b, tiles[0]), tag="bank%d" % bank)
             for n, t in enumerate(tiles):
-                members = keep.tile([P, 4 * BLOCK], F32, name="members%d_%d" % (b, t), tag="members", bufs=6)
+                members = keep.tile([P, 4 * BLOCK], F32, name="members%d_%d" % (b, t), tag="members", bufs=16)
                 if (b, t) in ON_VECTOR:
                     nc.vector.tensor_copy(members[:].bitcast(U32).rearrange("p (u j e) -> p j u e", u=2, e=2), ex[t][:].bitcast(U32).indirect(entries))
                     parts = [members[:, 2 * BLOCK * u + e : 2 * BLOCK * (u + 1) : 2] for u in range(2) for e in range(2)]
@@ -159,7 +159,7 @@ def tile_picked_mixhgsharegap_none_p_kernel(tc, x_words, x_scales, w1, gn, w2, w
             inverse = keep.tile([P, width], F32, name="inverse%d_%d" % (b, tiles[0]))
             nc.scalar.activation(inverse[:], root[:], ACT.Square)
             if b not in shares:
-                shares[b] = psum.tile([P, PACK, BLOCK], F32, name="share%d" % b, tag="bank%d" % (1 + b % 3))
+                shares[b] = psum.tile([P, PACK, BLOCK], F32, name="share%d" % b, tag="bank%d" % (4 + b))
             for n, t in enumerate(tiles):
                 nc.tensor.transpose(shares[b][:, t, :], inverse[:, P * n : P * (n + 1)], ident[:])
 
@@ -171,7 +171,7 @@ def tile_picked_mixhgsharegap_none_p_kernel(tc, x_words, x_scales, w1, gn, w2, w
             )
 
         def open_bank(t):
-            h_acc[t] = psum.tile([P, 3 * BLOCK], F32, name="h_acc%d" % t, tag="bank%d" % (4, 5, 6, 2)[t])
+            h_acc[t] = psum.tile([P, 3 * BLOCK], F32, name="h_acc%d" % t, tag="bank%d" % t)
             product(t, h_acc[t][:, : 2 * BLOCK], w3_codes, w3_scales, hz_codes, hz_scales, slice(0, 2 * BLOCK), True, False)
             product(t, h_acc[t][:, 2 * BLOCK :], w3_codes, w3_scales, hz_codes, hz_scales, slice(2 * BLOCK, 3 * BLOCK), False, False)
 
@@ -190,41 +190,33 @@ def tile_picked_mixhgsharegap_none_p_kernel(tc, x_words, x_scales, w1, gn, w2, w
 
         every = (0, 1, 2, 3)
         first_two, third, late = slice(0, 2 * BLOCK), slice(2 * BLOCK, 3 * BLOCK), slice(last * BLOCK, S)
-        fetch(0, every, 4)
-        fetch(1, every, 5)
         w3_bf = round_weight(w3_raw, "w3_bf")
+        w3_codes, w3_scales = quantise_weight(w3_bf, "w3")
+        for t in range(PACK):
+            open_bank(t)
+        for b in range(blocks):
+            fetch(b, every, 4 + b)
         for t in range(PACK):
             nc.vector.tensor_scalar(gained[:, t, :], ex[t][:, :S], gain[:, t : t + 1], None, ALU.mult)
-        w3_codes, w3_scales = quantise_weight(w3_bf, "w3")
-        invert(0, every)
-        fetch(2, every, 6)
-        open_bank(0)
         w2_bf = round_weight(w2_raw, "w2_bf")
-        invert(1, every)
-        open_bank(1)
         w2_codes, w2_scales = quantise_weight(w2_bf, "w2")
+        invert(0, every)
+        invert(1, every)
         weave(0)
         invert(2, every)
-        fetch(3, (0, 1), 7)
         weave(1)
-        open_bank(2)
-        fetch(3, (2, 3), 0)
-        open_bank(3)
-        quantise_z(first_two)
+        invert(3, every)
+        weave(2)
+        quantise_z(slice(0, 3 * BLOCK))
         for t in range(PACK):
             product(t, h_acc[t][:, first_two], w2_codes, w2_scales, z_codes, z_scales, first_two, False, False)
-        weave(2)
-        invert(3, (0, 1))
-        invert(3, (2, 3))
-        quantise_z(third)
-        for t in range(PACK):
             product(t, h_acc[t][:, third], w2_codes, w2_scales, z_codes, z_scales, third, False, True)
         weave(3)
         quantise_z(late)
         for t in range(PACK):
             nc.scalar.copy(h[t][:, : 3 * BLOCK], h_acc[t][:])
         for u in range(2):
-            h_late = psum.tile([P, 2, BLOCK], F32, name="h_late%d" % u, tag="bank%d" % (7, 0)[u])
+            h_late = psum.tile([P, 2, BLOCK], F32, name="h_late%d" % u, tag="bank%d" % (5 + u))
             for n in range(2):
                 product(2 * u + n, h_late[:, n, :], w3_codes, w3_scales, hz_codes, hz_scales, late, n == 0, False)
             for n in range(2):

@@ -3,8 +3,8 @@ from contextlib import ExitStack
 import concourse.mybir as mybir
 from concourse.masks import make_identity
 
-K, T, S, N, H, W = 512, 2048, 512, 512, 512, 2048
-FLOPS = 3 * 2 * 512 * 512 * 512
+K, T, S, N, H = 512, 2048, 512, 512, 512
+FLOPS = 2 * S * (K * H + H * N + K * N)
 
 F32 = mybir.dt.float32
 BF16 = mybir.dt.bfloat16
@@ -18,54 +18,62 @@ ALU = mybir.AluOpType
 
 P = 128
 PACK = 4
+MEMBERS = 4
 BLOCK = 128
+BLOCKS = S // BLOCK
+HALF = S // 2
+ENTRIES_PER_COLUMN = 16
 SPARE = 192
-ON_VECTOR = {(b, t) for b, n in enumerate((2, 2, 2, 3)) for t in range(4 - n, 4)}
-PAIRED = set()
+OUTER_TILES = (0, PACK - 1)
+PAIRED_FROM_BLOCK = 2
+BOTH_ON_SCALAR = 2
 
 
 def tile_picked_mixhgsharegap_none_p_kernel(tc, x_words, x_scales, w1, gn, w2, w3, offs, n1, hz, n2, n3, out):
     nc = tc.nc
-    blocks = S // BLOCK
     with ExitStack() as ctx:
         keep = ctx.enter_context(tc.tile_pool(name="keep", bufs=1))
         psum = ctx.enter_context(tc.psum_pool(name="psum", bufs=1))
 
-        def load_list(src, name):
-            lst = keep.tile(list(src.shape), U16, name=name)
-            nc.sync.dma_start(lst[:], src)
-            return lst
+        def bank(name, number):
+            return psum.tile([P, S], F32, name=name, tag="bank%d" % number)
 
-        def load_weight(w, name):
-            raw = keep.tile([P, PACK, 512], F32, name=name)
-            nc.sync.dma_start(raw[:], w.rearrange("(p j) c -> p j c", j=PACK))
+        def load_list(src, name):
+            offsets = keep.tile(list(src.shape), U16, name=name)
+            nc.sync.dma_start(offsets[:], src)
+            return offsets
+
+        def load_rows(w, cols, name):
+            raw = keep.tile([P, PACK, cols.stop - cols.start], F32, name=name)
+            nc.sync.dma_start(raw[:], w.rearrange("(p j) c -> p j c", j=PACK)[:, :, cols])
             return raw
 
-        def round_weight(raw, name, on_scalar=0):
-            grouped = keep.tile([P, PACK, P, PACK], BF16, name=name, align_bytes=64)
-            dst = grouped[:].rearrange("p t m j -> p m t j")
-            src = raw[:].rearrange("p j (m t) -> p m t j", t=PACK)
-            if on_scalar:
-                nc.scalar.copy(dst[:, :on_scalar], src[:, :on_scalar])
-            nc.vector.tensor_copy(dst[:, on_scalar:], src[:, on_scalar:])
-            return grouped
+        def round_and_deal(move, dealt, raw):
+            move(dealt.rearrange("p t m j -> p m t j"), raw[:].rearrange("p j (m t) -> p m t j", t=PACK))
 
-        def quantise_weight(grouped, name):
-            codes = keep.tile([P, 512], U32, name=name + "_codes", align_bytes=64)
-            scales = keep.tile([P, 512], U8, name=name + "_scales", align_bytes=64)
-            nc.vector.quantize_mx(
-                out=codes[:].bitcast(FP8X4), scales=scales[:], in_=grouped[:].rearrange("p t m j -> p (t m j)")
-            )
+        def quantise_weight(dealt, name):
+            codes = keep.tile([P, PACK * P], U32, name=name + "_codes", align_bytes=64)
+            scales = keep.tile([P, PACK * P], U8, name=name + "_scales", align_bytes=64)
+            nc.vector.quantize_mx(out=codes[:].bitcast(FP8X4), scales=scales[:], in_=dealt[:].rearrange("p t m j -> p (t m j)"))
             return codes, scales
+
+        def product(acc, weight, t, moving, cols, start, stop):
+            rows = slice(P * t, P * (t + 1))
+            nc.tensor.matmul_mx(
+                out=acc[:, cols],
+                lhsT=weight[0][:, rows].bitcast(FP8X4),
+                lhsT_scale=weight[1][:, rows],
+                rhs=moving[0][:, cols].bitcast(FP8X4),
+                rhs_scale=moving[1][:, cols],
+                start=start,
+                stop=stop,
+            )
 
         staged_scales = keep.tile([P, T], U8, name="staged_scales")
         for r in range(4):
             nc.sync.dma_start(staged_scales[r:P:32, :].bitcast(I32), x_scales[0, r:16:4, :].bitcast(I32))
         offs_sb = load_list(offs, "offs_sb")
-        w1_rows = w1.rearrange("(p j) c -> p j c", j=PACK)
-        w1_raw = [keep.tile([P, PACK, 256], F32, name="w1_raw%d" % u) for u in range(2)]
-        for u in range(2):
-            nc.sync.dma_start(w1_raw[u][:], w1_rows[:, :, 256 * u : 256 * (u + 1)])
+        w1_raw = [load_rows(w1, slice(H // 2 * u, H // 2 * (u + 1)), "w1_raw%d" % u) for u in range(2)]
         hz_sb = load_list(hz, "hz_sb")
         table_scales = keep.tile([P, T], U8, name="table_scales")
         nc.vector.memset(table_scales[:].bitcast(I32), 0)
@@ -79,10 +87,10 @@ def tile_picked_mixhgsharegap_none_p_kernel(tc, x_words, x_scales, w1, gn, w2, w
         table_words = keep.tile([P, T], U32, name="table_words")
         nc.sync.dma_start(table_words[:].bitcast(I32), x_words[0].rearrange("p c r -> p (c r)").bitcast(I32))
         n1_sb = load_list(n1, "n1_sb")
-        w3_raw = load_weight(w3, "w3_raw")
+        w3_raw = load_rows(w3, slice(0, N), "w3_raw")
         gain = keep.tile([P, PACK], F32, name="gain")
         nc.sync.dma_start(gain[:], gn.rearrange("(p t) o -> p (t o)", t=PACK))
-        w2_raw = load_weight(w2, "w2_raw")
+        w2_raw = load_rows(w2, slice(0, N), "w2_raw")
         n3_sb = load_list(n3, "n3_sb")
         n2_sb = load_list(n2, "n2_sb")
 
@@ -91,157 +99,140 @@ def tile_picked_mixhgsharegap_none_p_kernel(tc, x_words, x_scales, w1, gn, w2, w
             nc.gpsimd.memset(ex[t][:, S:], 0.0)
         hz_scales = keep.tile([P, S], U8, name="hz_scales", align_bytes=64)
         nc.gpsimd.memset(hz_scales[:], 0)
-
         ident = keep.tile([P, P], F32, name="ident")
         make_identity(nc, ident[:])
 
-        x_sc = keep.tile([P, S], U8, name="x_sc", align_bytes=64)
-        nc.vector.tensor_copy(x_sc[:], table_scales[:].indirect(offs_sb[:]))
-        w1_bf = keep.tile([P, PACK, P, PACK], BF16, name="w1_bf", align_bytes=64)
+        x_picked_scales = keep.tile([P, S], U8, name="x_picked_scales", align_bytes=64)
+        nc.vector.tensor_copy(x_picked_scales[:], table_scales[:].indirect(offs_sb[:]))
+        w1_dealt = keep.tile([P, PACK, P, PACK], BF16, name="w1_dealt", align_bytes=64)
         for u in range(2):
-            nc.scalar.copy(
-                w1_bf[:, :, 64 * u : 64 * (u + 1), :].rearrange("p t m j -> p m t j"),
-                w1_raw[u][:].rearrange("p j (m t) -> p m t j", t=PACK),
-            )
-        w1_codes, w1_scales = quantise_weight(w1_bf, "w1")
-        x_codes = keep.tile([P, S], U32, name="x_codes", align_bytes=64)
-        nc.vector.tensor_copy(x_codes[:], table_words[:].indirect(offs_sb[:]))
-        hz_sc_raw = keep.tile([P, S], U8, name="hz_sc_raw")
-        nc.vector.tensor_copy(hz_sc_raw[:], run_scales[:].indirect(hz_sb[:]))
-        for dst, src in ((0, 0), (1, 1), (2, 16), (3, 17)):
-            nc.sync.dma_start(hz_scales[dst:P:32, :].bitcast(I32), hz_sc_raw[src:P:32, :].bitcast(I32))
+            round_and_deal(nc.scalar.copy, w1_dealt[:, :, P // 2 * u : P // 2 * (u + 1), :], w1_raw[u])
+        w1_mx = quantise_weight(w1_dealt, "w1")
+        x_picked_words = keep.tile([P, S], U32, name="x_picked_words", align_bytes=64)
+        nc.vector.tensor_copy(x_picked_words[:], table_words[:].indirect(offs_sb[:]))
+        x_mx = (x_picked_words, x_picked_scales)
+        run_picked_scales = keep.tile([P, S], U8, name="run_picked_scales")
+        nc.vector.tensor_copy(run_picked_scales[:], run_scales[:].indirect(hz_sb[:]))
+        for r in range(4):
+            nc.sync.dma_start(hz_scales[r:P:32, :].bitcast(I32), run_picked_scales[16 * (r // 2) + r % 2 : P : 32, :].bitcast(I32))
+        hz_words = keep.tile([P, S], U32, name="hz_words", align_bytes=64)
+        nc.vector.tensor_copy(hz_words[:], table_words[:].indirect(hz_sb[:]))
+        hz_mx = (hz_words, hz_scales)
+
+        sums = [bank("sums%d" % b, PACK + b) for b in range(BLOCKS)]
+
+        def on_scalar(b, t):
+            return t in OUTER_TILES and (b, t) != (BLOCKS - 1, PACK - 1)
+
+        def fetch_and_sum(b, t):
+            width = MEMBERS * BLOCK // ENTRIES_PER_COLUMN
+            entries = n1_sb[:, width * b : width * (b + 1)]
+            members = keep.tile([P, MEMBERS * BLOCK], F32, name="members%d_%d" % (b, t))
+            if on_scalar(b, t):
+                nc.scalar.activation(members[:], ex[t][:].indirect(entries), ACT.Copy)
+                terms = [members[:, u::MEMBERS] for u in range(MEMBERS)]
+            else:
+                nc.vector.tensor_copy(
+                    members[:].bitcast(U32).rearrange("p (u j e) -> p j u e", u=2, e=2), ex[t][:].bitcast(U32).indirect(entries)
+                )
+                terms = [members[:, 2 * BLOCK * u + e : 2 * BLOCK * (u + 1) : 2] for u in range(2) for e in range(2)]
+            if t == 0 and b >= PAIRED_FROM_BLOCK:
+                pairs = keep.tile([P, 2 * BLOCK], F32, name="pairs%d" % b)
+                nc.vector.tensor_tensor(
+                    pairs[:].rearrange("p (u j) -> p j u", u=2),
+                    members[:, 0::2].rearrange("p (j u) -> p j u", u=2),
+                    members[:, 1::2].rearrange("p (j u) -> p j u", u=2),
+                    ALU.add,
+                )
+                terms = [pairs[:, BLOCK * u : BLOCK * (u + 1)] for u in range(2)]
+            for n, term in enumerate(terms):
+                nc.tensor.matmul(
+                    sums[b][:, P * t : P * (t + 1)], lhsT=term, rhs=ident[:], is_transpose=True, start=(n == 0), stop=(n == len(terms) - 1)
+                )
 
         for t in range(PACK):
-            y = psum.tile([P, S], F32, name="y%d" % t, tag="bank%d" % t)
-            cols = slice(P * t, P * (t + 1))
-            nc.tensor.matmul_mx(
-                out=y[:], lhsT=w1_codes[:, cols].bitcast(FP8X4), lhsT_scale=w1_scales[:, cols],
-                rhs=x_codes[:].bitcast(FP8X4), rhs_scale=x_sc[:], start=True, stop=True,
-            )
+            y = bank("y%d" % t, t)
+            product(y, w1_mx, t, x_mx, slice(0, S), True, True)
             nc.scalar.activation(ex[t][:, :S], y[:], ACT.Exp, scale=0.5)
+            if on_scalar(0, t):
+                fetch_and_sum(0, t)
 
-        hz_codes = keep.tile([P, S], U32, name="hz_codes", align_bytes=64)
-        nc.vector.tensor_copy(hz_codes[:], table_words[:].indirect(hz_sb[:]))
-
-        z_codes = keep.tile([P, S], U32, name="z_codes", align_bytes=64)
-        z_scales = keep.tile([P, S], U8, name="z_scales", align_bytes=64)
-        h_acc = {}
-        gained = keep.tile([P, PACK, S], F32, name="gained")
-        h = [keep.tile([P, S], F32, name="h%d" % t) for t in range(PACK)]
-        totals, shares = {}, {}
-        last = blocks - 1
-
-        def fetch(b, tiles, bank):
-            entries = n1_sb[:, 32 * b : 32 * (b + 1)]
-            total = psum.tile([P, len(tiles), P], F32, name="total%d_%d" % (b, tiles[0]), tag="bank%d" % bank)
-            for n, t in enumerate(tiles):
-                members = keep.tile([P, 4 * BLOCK], F32, name="members%d_%d" % (b, t), tag="members", bufs=16)
-                if (b, t) in ON_VECTOR:
-                    nc.vector.tensor_copy(members[:].bitcast(U32).rearrange("p (u j e) -> p j u e", u=2, e=2), ex[t][:].bitcast(U32).indirect(entries))
-                    parts = [members[:, 2 * BLOCK * u + e : 2 * BLOCK * (u + 1) : 2] for u in range(2) for e in range(2)]
-                else:
-                    nc.scalar.activation(members[:], ex[t][:].indirect(entries), ACT.Copy)
-                    parts = [members[:, u::4] for u in range(4)]
-                if (b, t) in PAIRED:
-                    pairs = keep.tile([P, 2 * BLOCK], F32, name="pairs%d_%d" % (b, t))
-                    nc.vector.tensor_tensor(pairs[:].rearrange("p (u j) -> p j u", u=2), members[:, 0::2].rearrange("p (j u) -> p j u", u=2), members[:, 1::2].rearrange("p (j u) -> p j u", u=2), ALU.add)
-                    parts = [pairs[:, BLOCK * u : BLOCK * (u + 1)] for u in range(2)]
-                for u, part in enumerate(parts):
-                    nc.tensor.matmul(
-                        total[:, n, :], lhsT=part, rhs=ident[:], is_transpose=True, start=(u == 0), stop=(u == len(parts) - 1)
-                    )
-            totals[b, tiles[0]] = total
-
-        def invert(b, tiles):
-            width = len(tiles) * P
-            root = keep.tile([P, width], F32, name="root%d_%d" % (b, tiles[0]))
-            nc.scalar.activation(root[:], totals[b, tiles[0]][:].rearrange("p t m -> p (t m)"), ACT.Abs_reciprocal_sqrt, scale=0.25, bias=0.125)
-            inverse = keep.tile([P, width], F32, name="inverse%d_%d" % (b, tiles[0]))
-            nc.scalar.activation(inverse[:], root[:], ACT.Square)
-            if b not in shares:
-                shares[b] = psum.tile([P, PACK, BLOCK], F32, name="share%d" % b, tag="bank%d" % (4 + b))
-            for n, t in enumerate(tiles):
-                nc.tensor.transpose(shares[b][:, t, :], inverse[:, P * n : P * (n + 1)], ident[:])
-
-        def product(t, acc, codes, scales, rhs_codes, rhs_scales, cols, start, stop):
-            rows = slice(P * t, P * (t + 1))
-            nc.tensor.matmul_mx(
-                out=acc, lhsT=codes[:, rows].bitcast(FP8X4), lhsT_scale=scales[:, rows],
-                rhs=rhs_codes[:, cols].bitcast(FP8X4), rhs_scale=rhs_scales[:, cols], start=start, stop=stop,
-            )
-
-        def open_bank(t):
-            h_acc[t] = psum.tile([P, 3 * BLOCK], F32, name="h_acc%d" % t, tag="bank%d" % t)
-            product(t, h_acc[t][:, : 2 * BLOCK], w3_codes, w3_scales, hz_codes, hz_scales, slice(0, 2 * BLOCK), True, False)
-            product(t, h_acc[t][:, 2 * BLOCK :], w3_codes, w3_scales, hz_codes, hz_scales, slice(2 * BLOCK, 3 * BLOCK), False, False)
-
-        woven = keep.tile([P, S, PACK], BF16, name="z_woven", align_bytes=64)
-
-        def weave(b):
-            cols = slice(BLOCK * b, BLOCK * (b + 1))
-            nc.vector.tensor_tensor(
-                woven[:, cols, :], shares[b][:].rearrange("p t j -> p j t"), gained[:, :, cols].rearrange("p t j -> p j t"), ALU.mult
-            )
-
-        def quantise_z(cols):
-            nc.vector.quantize_mx(
-                out=z_codes[:, cols].bitcast(FP8X4), scales=z_scales[:, cols], in_=woven[:, cols, :].rearrange("p j t -> p (j t)")
-            )
-
-        every = (0, 1, 2, 3)
-        first_two, third, late = slice(0, 2 * BLOCK), slice(2 * BLOCK, 3 * BLOCK), slice(last * BLOCK, S)
-        w3_bf = round_weight(w3_raw, "w3_bf")
-        w3_codes, w3_scales = quantise_weight(w3_bf, "w3")
+        w3_dealt = keep.tile([P, PACK, P, PACK], BF16, name="w3_dealt", align_bytes=64)
+        round_and_deal(nc.vector.tensor_copy, w3_dealt[:], w3_raw)
+        w3_mx = quantise_weight(w3_dealt, "w3")
+        h_acc = [bank("h_acc%d" % t, t) for t in range(PACK)]
         for t in range(PACK):
-            open_bank(t)
-        for b in range(blocks):
-            fetch(b, every, 4 + b)
+            product(h_acc[t], w3_mx, t, hz_mx, slice(0, S), True, False)
+
+        for b in range(BLOCKS):
+            for t in range(PACK):
+                if b > 0 or not on_scalar(b, t):
+                    fetch_and_sum(b, t)
+        gained = keep.tile([P, PACK, S], F32, name="gained")
         for t in range(PACK):
             nc.vector.tensor_scalar(gained[:, t, :], ex[t][:, :S], gain[:, t : t + 1], None, ALU.mult)
-        w2_bf = round_weight(w2_raw, "w2_bf")
-        w2_codes, w2_scales = quantise_weight(w2_bf, "w2")
-        invert(0, every)
-        invert(1, every)
-        weave(0)
-        invert(2, every)
-        weave(1)
-        invert(3, every)
-        weave(2)
-        quantise_z(slice(0, 3 * BLOCK))
-        for t in range(PACK):
-            product(t, h_acc[t][:, first_two], w2_codes, w2_scales, z_codes, z_scales, first_two, False, False)
-            product(t, h_acc[t][:, third], w2_codes, w2_scales, z_codes, z_scales, third, False, True)
-        weave(3)
-        quantise_z(late)
-        for t in range(PACK):
-            nc.scalar.copy(h[t][:, : 3 * BLOCK], h_acc[t][:])
-        for u in range(2):
-            h_late = psum.tile([P, 2, BLOCK], F32, name="h_late%d" % u, tag="bank%d" % (5 + u))
-            for n in range(2):
-                product(2 * u + n, h_late[:, n, :], w3_codes, w3_scales, hz_codes, hz_scales, late, n == 0, False)
-            for n in range(2):
-                product(2 * u + n, h_late[:, n, :], w2_codes, w2_scales, z_codes, z_scales, late, False, n == 1)
-            for n in range(2):
-                if u == 0:
-                    nc.vector.tensor_copy(h[2 * u + n][:, late], h_late[:, n, :])
-                else:
-                    nc.scalar.copy(h[2 * u + n][:, late], h_late[:, n, :])
+        w2_dealt = keep.tile([P, PACK, P, PACK], BF16, name="w2_dealt", align_bytes=64)
+        round_and_deal(nc.vector.tensor_copy, w2_dealt[:], w2_raw)
+        w2_mx = quantise_weight(w2_dealt, "w2")
 
+        z_rounded = keep.tile([P, S, PACK], BF16, name="z_rounded", align_bytes=64)
+        z_codes = keep.tile([P, S], U32, name="z_codes", align_bytes=64)
+        z_scales = keep.tile([P, S], U8, name="z_scales", align_bytes=64)
+        inverses = {}
+
+        def invert(b):
+            root = keep.tile([P, S], F32, name="root%d" % b)
+            nc.scalar.activation(root[:], sums[b][:], ACT.Abs_reciprocal_sqrt, scale=0.25, bias=0.125)
+            turned = keep.tile([P, S], F32, name="turned%d" % b)
+            nc.scalar.activation(turned[:], root[:], ACT.Square)
+            inverses[b] = bank("inverse%d" % b, PACK + b)
+            for t in range(PACK):
+                nc.tensor.transpose(inverses[b][:, P * t : P * (t + 1)], turned[:, P * t : P * (t + 1)], ident[:])
+
+        def make_z(b):
+            cols = slice(BLOCK * b, BLOCK * (b + 1))
+            nc.vector.tensor_tensor(
+                z_rounded[:, cols, :],
+                inverses[b][:].rearrange("p (t j) -> p j t", t=PACK),
+                gained[:, :, cols].rearrange("p t j -> p j t"),
+                ALU.mult,
+            )
+
+        def multiply_z(u):
+            cols = slice(HALF * u, HALF * (u + 1))
+            nc.vector.quantize_mx(
+                out=z_codes[:, cols].bitcast(FP8X4), scales=z_scales[:, cols], in_=z_rounded[:, cols, :].rearrange("p j t -> p (j t)")
+            )
+            for t in range(PACK):
+                product(h_acc[t], w2_mx, t, (z_codes, z_scales), cols, False, u == 1)
+
+        invert(0)
+        for b in range(BLOCKS):
+            if b + 1 < BLOCKS:
+                invert(b + 1)
+            make_z(b)
+            if b % 2 == 1:
+                multiply_z(b // 2)
+
+        h = [keep.tile([P, S], F32, name="h%d" % t) for t in range(PACK)]
+        for t in range(PACK):
+            move = nc.vector.tensor_copy if t % 2 == 1 else nc.scalar.copy
+            move(h[t][:], h_acc[t][:])
         out_rows = out.rearrange("(p t) j -> p t j", t=PACK)
-        half = S // 2
-        units = [(t, u) for t in range(PACK) for u in range(2)]
-        for n, (t, u) in enumerate(units):
-            entries = slice(16 * u, 16 * (u + 1))
-            second = keep.tile([P, half], F32, name="second%d" % n)
-            nc.scalar.activation(second[:], h[t][:].indirect(n3_sb[:, entries]), ACT.Copy)
-            gap = keep.tile([P, half], F32, name="gap%d" % n)
-            if n == 0 or n >= 6:
-                first = keep.tile([P, half], F32, name="first%d" % n)
-                if n == 0:
-                    nc.vector.tensor_copy(first[:], h[t][:].indirect(n2_sb[:, entries]))
-                else:
-                    nc.scalar.activation(first[:], h[t][:].indirect(n2_sb[:, entries]), ACT.Copy)
-                nc.vector.tensor_tensor(gap[:], first[:], second[:], ALU.subtract)
-            else:
-                nc.vector.tensor_tensor(gap[:], h[t][:].indirect(n2_sb[:, entries]), second[:], ALU.subtract)
-            nc.sync.dma_start(out_rows[:, t, half * u : half * (u + 1)], gap[:])
+        pieces = [(t, u) for t in range(PACK) for u in range(2)]
+        for n, (t, u) in enumerate(pieces):
+            entries = slice(HALF // ENTRIES_PER_COLUMN * u, HALF // ENTRIES_PER_COLUMN * (u + 1))
+            at_n3 = keep.tile([P, HALF], F32, name="at_n3_%d" % n)
+            nc.scalar.activation(at_n3[:], h[t][:].indirect(n3_sb[:, entries]), ACT.Copy)
+            at_n2 = h[t][:].indirect(n2_sb[:, entries])
+            if n == 0:
+                fetched = keep.tile([P, HALF], F32, name="at_n2_%d" % n)
+                nc.vector.tensor_copy(fetched[:], at_n2)
+                at_n2 = fetched[:]
+            elif n >= len(pieces) - BOTH_ON_SCALAR:
+                fetched = keep.tile([P, HALF], F32, name="at_n2_%d" % n)
+                nc.scalar.activation(fetched[:], at_n2, ACT.Copy)
+                at_n2 = fetched[:]
+            gap = keep.tile([P, HALF], F32, name="gap%d" % n)
+            nc.vector.tensor_tensor(gap[:], at_n2, at_n3[:], ALU.subtract)
+            nc.sync.dma_start(out_rows[:, t, HALF * u : HALF * (u + 1)], gap[:])

@@ -23,9 +23,8 @@ BLOCK = 128
 BLOCKS = S // BLOCK
 HALF = S // 2
 ENTRIES_PER_COLUMN = 16
-SPARE = 192
-OUTER_TILES = (0, PACK - 1)
-PAIRED_FROM_BLOCK = 2
+SPARE = 32
+TILES_ON_VECTOR = (2, 2, 2, 3)
 BOTH_ON_SCALAR = 2
 
 
@@ -35,32 +34,40 @@ def tile_picked_mixhgsharegap_none_p_kernel(tc, x_words, x_scales, w1, gn, w2, w
         keep = ctx.enter_context(tc.tile_pool(name="keep", bufs=1))
         psum = ctx.enter_context(tc.psum_pool(name="psum", bufs=1))
 
-        def bank(name, number):
-            return psum.tile([P, S], F32, name=name, tag="bank%d" % number)
+        def bank(shape, name, number):
+            return psum.tile(shape, F32, name=name, tag="bank%d" % number)
 
         def load_list(src, name):
             offsets = keep.tile(list(src.shape), U16, name=name)
             nc.sync.dma_start(offsets[:], src)
             return offsets
 
-        def load_rows(w, cols, name):
-            raw = keep.tile([P, PACK, cols.stop - cols.start], F32, name=name)
-            nc.sync.dma_start(raw[:], w.rearrange("(p j) c -> p j c", j=PACK)[:, :, cols])
+        def rows_by_partition(w):
+            return w.rearrange("(p j) c -> p j c", j=PACK)
+
+        def load_weight(w, name):
+            raw = keep.tile([P, PACK, N], F32, name=name)
+            nc.sync.dma_start(raw[:], rows_by_partition(w))
             return raw
 
         def round_and_deal(move, dealt, raw):
             move(dealt.rearrange("p t m j -> p m t j"), raw[:].rearrange("p j (m t) -> p m t j", t=PACK))
 
-        def quantise_weight(dealt, name):
+        def quantise_dealt(dealt, name):
             codes = keep.tile([P, PACK * P], U32, name=name + "_codes", align_bytes=64)
             scales = keep.tile([P, PACK * P], U8, name=name + "_scales", align_bytes=64)
             nc.vector.quantize_mx(out=codes[:].bitcast(FP8X4), scales=scales[:], in_=dealt[:].rearrange("p t m j -> p (t m j)"))
             return codes, scales
 
+        def quantise_weight(raw, name):
+            dealt = keep.tile([P, PACK, P, PACK], BF16, name=name + "_dealt", align_bytes=64)
+            round_and_deal(nc.vector.tensor_copy, dealt[:], raw)
+            return quantise_dealt(dealt, name)
+
         def product(acc, weight, t, moving, cols, start, stop):
             rows = slice(P * t, P * (t + 1))
             nc.tensor.matmul_mx(
-                out=acc[:, cols],
+                out=acc,
                 lhsT=weight[0][:, rows].bitcast(FP8X4),
                 lhsT_scale=weight[1][:, rows],
                 rhs=moving[0][:, cols].bitcast(FP8X4),
@@ -73,7 +80,9 @@ def tile_picked_mixhgsharegap_none_p_kernel(tc, x_words, x_scales, w1, gn, w2, w
         for r in range(4):
             nc.sync.dma_start(staged_scales[r:P:32, :].bitcast(I32), x_scales[0, r:16:4, :].bitcast(I32))
         offs_sb = load_list(offs, "offs_sb")
-        w1_raw = [load_rows(w1, slice(H // 2 * u, H // 2 * (u + 1)), "w1_raw%d" % u) for u in range(2)]
+        w1_raw = [keep.tile([P, PACK, H // 2], F32, name="w1_raw%d" % u) for u in range(2)]
+        for u in range(2):
+            nc.sync.dma_start(w1_raw[u][:], rows_by_partition(w1)[:, :, H // 2 * u : H // 2 * (u + 1)])
         hz_sb = load_list(hz, "hz_sb")
         table_scales = keep.tile([P, T], U8, name="table_scales")
         nc.vector.memset(table_scales[:].bitcast(I32), 0)
@@ -87,10 +96,10 @@ def tile_picked_mixhgsharegap_none_p_kernel(tc, x_words, x_scales, w1, gn, w2, w
         table_words = keep.tile([P, T], U32, name="table_words")
         nc.sync.dma_start(table_words[:].bitcast(I32), x_words[0].rearrange("p c r -> p (c r)").bitcast(I32))
         n1_sb = load_list(n1, "n1_sb")
-        w3_raw = load_rows(w3, slice(0, N), "w3_raw")
+        w3_raw = load_weight(w3, "w3_raw")
         gain = keep.tile([P, PACK], F32, name="gain")
         nc.sync.dma_start(gain[:], gn.rearrange("(p t) o -> p (t o)", t=PACK))
-        w2_raw = load_rows(w2, slice(0, N), "w2_raw")
+        w2_raw = load_weight(w2, "w2_raw")
         n3_sb = load_list(n3, "n3_sb")
         n2_sb = load_list(n2, "n2_sb")
 
@@ -102,128 +111,113 @@ def tile_picked_mixhgsharegap_none_p_kernel(tc, x_words, x_scales, w1, gn, w2, w
         ident = keep.tile([P, P], F32, name="ident")
         make_identity(nc, ident[:])
 
-        x_picked_scales = keep.tile([P, S], U8, name="x_picked_scales", align_bytes=64)
-        nc.vector.tensor_copy(x_picked_scales[:], table_scales[:].indirect(offs_sb[:]))
+        offs_scales = keep.tile([P, S], U8, name="offs_scales", align_bytes=64)
+        nc.vector.tensor_copy(offs_scales[:], table_scales[:].indirect(offs_sb[:]))
         w1_dealt = keep.tile([P, PACK, P, PACK], BF16, name="w1_dealt", align_bytes=64)
         for u in range(2):
             round_and_deal(nc.scalar.copy, w1_dealt[:, :, P // 2 * u : P // 2 * (u + 1), :], w1_raw[u])
-        w1_mx = quantise_weight(w1_dealt, "w1")
-        x_picked_words = keep.tile([P, S], U32, name="x_picked_words", align_bytes=64)
-        nc.vector.tensor_copy(x_picked_words[:], table_words[:].indirect(offs_sb[:]))
-        x_mx = (x_picked_words, x_picked_scales)
-        run_picked_scales = keep.tile([P, S], U8, name="run_picked_scales")
-        nc.vector.tensor_copy(run_picked_scales[:], run_scales[:].indirect(hz_sb[:]))
+        w1_mx = quantise_dealt(w1_dealt, "w1")
+        offs_words = keep.tile([P, S], U32, name="offs_words", align_bytes=64)
+        nc.vector.tensor_copy(offs_words[:], table_words[:].indirect(offs_sb[:]))
+        picked_run_scales = keep.tile([P, S], U8, name="picked_run_scales")
+        nc.vector.tensor_copy(picked_run_scales[:], run_scales[:].indirect(hz_sb[:]))
         for r in range(4):
-            nc.sync.dma_start(hz_scales[r:P:32, :].bitcast(I32), run_picked_scales[16 * (r // 2) + r % 2 : P : 32, :].bitcast(I32))
+            nc.sync.dma_start(hz_scales[r:P:32, :].bitcast(I32), picked_run_scales[16 * (r // 2) + r % 2 : P : 32, :].bitcast(I32))
+
+        for t in range(PACK):
+            y = bank([P, S], "y%d" % t, t)
+            product(y[:], w1_mx, t, (offs_words, offs_scales), slice(0, S), True, True)
+            nc.scalar.activation(ex[t][:, :S], y[:], ACT.Exp, scale=0.5)
+
         hz_words = keep.tile([P, S], U32, name="hz_words", align_bytes=64)
         nc.vector.tensor_copy(hz_words[:], table_words[:].indirect(hz_sb[:]))
         hz_mx = (hz_words, hz_scales)
 
-        sums = [bank("sums%d" % b, PACK + b) for b in range(BLOCKS)]
-
-        def on_scalar(b, t):
-            return t in OUTER_TILES and (b, t) != (BLOCKS - 1, PACK - 1)
-
-        def fetch_and_sum(b, t):
-            width = MEMBERS * BLOCK // ENTRIES_PER_COLUMN
-            entries = n1_sb[:, width * b : width * (b + 1)]
-            members = keep.tile([P, MEMBERS * BLOCK], F32, name="members%d_%d" % (b, t))
-            if on_scalar(b, t):
-                nc.scalar.activation(members[:], ex[t][:].indirect(entries), ACT.Copy)
-                terms = [members[:, u::MEMBERS] for u in range(MEMBERS)]
-            else:
-                nc.vector.tensor_copy(
-                    members[:].bitcast(U32).rearrange("p (u j e) -> p j u e", u=2, e=2), ex[t][:].bitcast(U32).indirect(entries)
-                )
-                terms = [members[:, 2 * BLOCK * u + e : 2 * BLOCK * (u + 1) : 2] for u in range(2) for e in range(2)]
-            if t == 0 and b >= PAIRED_FROM_BLOCK:
-                pairs = keep.tile([P, 2 * BLOCK], F32, name="pairs%d" % b)
-                nc.vector.tensor_tensor(
-                    pairs[:].rearrange("p (u j) -> p j u", u=2),
-                    members[:, 0::2].rearrange("p (j u) -> p j u", u=2),
-                    members[:, 1::2].rearrange("p (j u) -> p j u", u=2),
-                    ALU.add,
-                )
-                terms = [pairs[:, BLOCK * u : BLOCK * (u + 1)] for u in range(2)]
-            for n, term in enumerate(terms):
-                nc.tensor.matmul(
-                    sums[b][:, P * t : P * (t + 1)], lhsT=term, rhs=ident[:], is_transpose=True, start=(n == 0), stop=(n == len(terms) - 1)
-                )
-
-        for t in range(PACK):
-            y = bank("y%d" % t, t)
-            product(y, w1_mx, t, x_mx, slice(0, S), True, True)
-            nc.scalar.activation(ex[t][:, :S], y[:], ACT.Exp, scale=0.5)
-            if on_scalar(0, t):
-                fetch_and_sum(0, t)
-
-        w3_dealt = keep.tile([P, PACK, P, PACK], BF16, name="w3_dealt", align_bytes=64)
-        round_and_deal(nc.vector.tensor_copy, w3_dealt[:], w3_raw)
-        w3_mx = quantise_weight(w3_dealt, "w3")
-        h_acc = [bank("h_acc%d" % t, t) for t in range(PACK)]
-        for t in range(PACK):
-            product(h_acc[t], w3_mx, t, hz_mx, slice(0, S), True, False)
-
-        for b in range(BLOCKS):
-            for t in range(PACK):
-                if b > 0 or not on_scalar(b, t):
-                    fetch_and_sum(b, t)
-        gained = keep.tile([P, PACK, S], F32, name="gained")
-        for t in range(PACK):
-            nc.vector.tensor_scalar(gained[:, t, :], ex[t][:, :S], gain[:, t : t + 1], None, ALU.mult)
-        w2_dealt = keep.tile([P, PACK, P, PACK], BF16, name="w2_dealt", align_bytes=64)
-        round_and_deal(nc.vector.tensor_copy, w2_dealt[:], w2_raw)
-        w2_mx = quantise_weight(w2_dealt, "w2")
-
-        z_rounded = keep.tile([P, S, PACK], BF16, name="z_rounded", align_bytes=64)
         z_codes = keep.tile([P, S], U32, name="z_codes", align_bytes=64)
         z_scales = keep.tile([P, S], U8, name="z_scales", align_bytes=64)
-        inverses = {}
+        z_mx = (z_codes, z_scales)
+        gained = keep.tile([P, PACK, S], F32, name="gained")
+        h = [keep.tile([P, S], F32, name="h%d" % t) for t in range(PACK)]
+        z_rounded = keep.tile([P, S, PACK], BF16, name="z_rounded", align_bytes=64)
+        h_early, sums, inverses = [], [], []
+
+        def fetch_and_sum(b):
+            width = MEMBERS * BLOCK // ENTRIES_PER_COLUMN
+            entries = n1_sb[:, width * b : width * (b + 1)]
+            sums.append(bank([P, PACK, P], "sums%d" % b, PACK + b))
+            for t in range(PACK):
+                members = keep.tile([P, MEMBERS * BLOCK], F32, name="members%d_%d" % (b, t), tag="members", bufs=BLOCKS * PACK)
+                if t >= PACK - TILES_ON_VECTOR[b]:
+                    nc.vector.tensor_copy(members[:], ex[t][:].indirect(entries))
+                else:
+                    nc.scalar.activation(members[:], ex[t][:].indirect(entries), ACT.Copy)
+                for u in range(MEMBERS):
+                    nc.tensor.matmul(
+                        sums[b][:, t, :], lhsT=members[:, u::MEMBERS], rhs=ident[:], is_transpose=True, start=(u == 0), stop=(u == MEMBERS - 1)
+                    )
 
         def invert(b):
-            root = keep.tile([P, S], F32, name="root%d" % b)
-            nc.scalar.activation(root[:], sums[b][:], ACT.Abs_reciprocal_sqrt, scale=0.25, bias=0.125)
-            turned = keep.tile([P, S], F32, name="turned%d" % b)
+            root = keep.tile([P, PACK * P], F32, name="root%d" % b)
+            nc.scalar.activation(root[:], sums[b][:].rearrange("j t p -> j (t p)"), ACT.Abs_reciprocal_sqrt, scale=0.25, bias=0.125)
+            turned = keep.tile([P, PACK * P], F32, name="turned%d" % b)
             nc.scalar.activation(turned[:], root[:], ACT.Square)
-            inverses[b] = bank("inverse%d" % b, PACK + b)
+            inverses.append(bank([P, PACK, BLOCK], "inverse%d" % b, PACK + b))
             for t in range(PACK):
-                nc.tensor.transpose(inverses[b][:, P * t : P * (t + 1)], turned[:, P * t : P * (t + 1)], ident[:])
+                nc.tensor.transpose(inverses[b][:, t, :], turned[:, P * t : P * (t + 1)], ident[:])
 
         def make_z(b):
             cols = slice(BLOCK * b, BLOCK * (b + 1))
             nc.vector.tensor_tensor(
-                z_rounded[:, cols, :],
-                inverses[b][:].rearrange("p (t j) -> p j t", t=PACK),
-                gained[:, :, cols].rearrange("p t j -> p j t"),
-                ALU.mult,
+                z_rounded[:, cols, :], inverses[b][:].rearrange("p t j -> p j t"), gained[:, :, cols].rearrange("p t j -> p j t"), ALU.mult
             )
 
-        def multiply_z(u):
-            cols = slice(HALF * u, HALF * (u + 1))
+        def quantise_z(cols):
             nc.vector.quantize_mx(
                 out=z_codes[:, cols].bitcast(FP8X4), scales=z_scales[:, cols], in_=z_rounded[:, cols, :].rearrange("p j t -> p (j t)")
             )
-            for t in range(PACK):
-                product(h_acc[t], w2_mx, t, (z_codes, z_scales), cols, False, u == 1)
 
-        invert(0)
-        for b in range(BLOCKS):
-            if b + 1 < BLOCKS:
-                invert(b + 1)
-            make_z(b)
-            if b % 2 == 1:
-                multiply_z(b // 2)
+        early, late = slice(0, S - BLOCK), slice(S - BLOCK, S)
+        early_passes = (slice(0, 2 * BLOCK), slice(2 * BLOCK, 3 * BLOCK))
 
-        h = [keep.tile([P, S], F32, name="h%d" % t) for t in range(PACK)]
+        w3_mx = quantise_weight(w3_raw, "w3")
         for t in range(PACK):
-            move = nc.vector.tensor_copy if t % 2 == 1 else nc.scalar.copy
-            move(h[t][:], h_acc[t][:])
+            h_early.append(bank([P, S - BLOCK], "h_early%d" % t, t))
+            for n, cols in enumerate(early_passes):
+                product(h_early[t][:, cols], w3_mx, t, hz_mx, cols, n == 0, False)
+
+        for b in range(BLOCKS):
+            fetch_and_sum(b)
+        for t in range(PACK):
+            nc.vector.tensor_scalar(gained[:, t, :], ex[t][:, :S], gain[:, t : t + 1], None, ALU.mult)
+        w2_mx = quantise_weight(w2_raw, "w2")
+        invert(0)
+        for b in range(BLOCKS - 1):
+            invert(b + 1)
+            make_z(b)
+        quantise_z(early)
+        for t in range(PACK):
+            for n, cols in enumerate(early_passes):
+                product(h_early[t][:, cols], w2_mx, t, z_mx, cols, False, n == len(early_passes) - 1)
+        make_z(BLOCKS - 1)
+        quantise_z(late)
+        for t in range(PACK):
+            nc.scalar.copy(h[t][:, early], h_early[t][:])
+        for u, move in enumerate((nc.vector.tensor_copy, nc.scalar.copy)):
+            h_late = bank([P, 2, BLOCK], "h_late%d" % u, PACK + 1 + u)
+            for n in range(2):
+                product(h_late[:, n, :], w3_mx, 2 * u + n, hz_mx, late, n == 0, False)
+            for n in range(2):
+                product(h_late[:, n, :], w2_mx, 2 * u + n, z_mx, late, False, n == 1)
+            for n in range(2):
+                move(h[2 * u + n][:, late], h_late[:, n, :])
+
         out_rows = out.rearrange("(p t) j -> p t j", t=PACK)
         pieces = [(t, u) for t in range(PACK) for u in range(2)]
         for n, (t, u) in enumerate(pieces):
             entries = slice(HALF // ENTRIES_PER_COLUMN * u, HALF // ENTRIES_PER_COLUMN * (u + 1))
             at_n3 = keep.tile([P, HALF], F32, name="at_n3_%d" % n)
             nc.scalar.activation(at_n3[:], h[t][:].indirect(n3_sb[:, entries]), ACT.Copy)
+            gap = keep.tile([P, HALF], F32, name="gap%d" % n)
             at_n2 = h[t][:].indirect(n2_sb[:, entries])
             if n == 0:
                 fetched = keep.tile([P, HALF], F32, name="at_n2_%d" % n)
@@ -233,6 +227,5 @@ def tile_picked_mixhgsharegap_none_p_kernel(tc, x_words, x_scales, w1, gn, w2, w
                 fetched = keep.tile([P, HALF], F32, name="at_n2_%d" % n)
                 nc.scalar.activation(fetched[:], at_n2, ACT.Copy)
                 at_n2 = fetched[:]
-            gap = keep.tile([P, HALF], F32, name="gap%d" % n)
             nc.vector.tensor_tensor(gap[:], at_n2, at_n3[:], ALU.subtract)
             nc.sync.dma_start(out_rows[:, t, HALF * u : HALF * (u + 1)], gap[:])

from contextlib import ExitStack

import concourse.mybir as mybir
from concourse.masks import make_identity

K, T, S, N, H = 512, 2048, 512, 512, 512
FLOPS = 2 * S * (K * H + H * N + K * N)

F32 = mybir.dt.float32
BF16 = mybir.dt.bfloat16
I32 = mybir.dt.int32
U32 = mybir.dt.uint32
U16 = mybir.dt.uint16
U8 = mybir.dt.uint8
FP8X4 = mybir.dt.float8_e4m3fn_x4
ACT = mybir.ActivationFunctionType
ALU = mybir.AluOpType

P = 128
PACK = 4
MEMBERS = 4
BLOCK = 128
BLOCKS = S // BLOCK
HALF = S // 2
ENTRIES_PER_COLUMN = 16
SPARE = 32
TILES_ON_VECTOR = (2, 2, 2, 3)
BOTH_ON_SCALAR = 2


def tile_picked_mixhgsharegap_none_p_kernel(tc, x_words, x_scales, w1, gn, w2, w3, offs, n1, hz, n2, n3, out):
    nc = tc.nc
    with ExitStack() as ctx:
        keep = ctx.enter_context(tc.tile_pool(name="keep", bufs=1))
        psum = ctx.enter_context(tc.psum_pool(name="psum", bufs=1))

        def bank(shape, name, number):
            return psum.tile(shape, F32, name=name, tag="bank%d" % number)

        def load_list(src, name):
            offsets = keep.tile(list(src.shape), U16, name=name)
            nc.sync.dma_start(offsets[:], src)
            return offsets

        def rows_by_partition(w):
            return w.rearrange("(p j) c -> p j c", j=PACK)

        def load_weight(w, name):
            raw = keep.tile([P, PACK, N], F32, name=name)
            nc.sync.dma_start(raw[:], rows_by_partition(w))
            return raw

        def round_and_deal(move, dealt, raw):
            move(dealt.rearrange("p t m j -> p m t j"), raw[:].rearrange("p j (m t) -> p m t j", t=PACK))

        def quantise_dealt(dealt, name):
            codes = keep.tile([P, PACK * P], U32, name=name + "_codes", align_bytes=64)
            scales = keep.tile([P, PACK * P], U8, name=name + "_scales", align_bytes=64)
            nc.vector.quantize_mx(out=codes[:].bitcast(FP8X4), scales=scales[:], in_=dealt[:].rearrange("p t m j -> p (t m j)"))
            return codes, scales

        def quantise_weight(raw, name):
            dealt = keep.tile([P, PACK, P, PACK], BF16, name=name + "_dealt", align_bytes=64)
            round_and_deal(nc.vector.tensor_copy, dealt[:], raw)
            return quantise_dealt(dealt, name)

        def product(acc, weight, t, moving, cols, start, stop):
            rows = slice(P * t, P * (t + 1))
            nc.tensor.matmul_mx(
                out=acc,
                lhsT=weight[0][:, rows].bitcast(FP8X4),
                lhsT_scale=weight[1][:, rows],
                rhs=moving[0][:, cols].bitcast(FP8X4),
                rhs_scale=moving[1][:, cols],
                start=start,
                stop=stop,
            )

        staged_scales = keep.tile([P, T], U8, name="staged_scales")
        for r in range(4):
            nc.sync.dma_start(staged_scales[r:P:32, :].bitcast(I32), x_scales[0, r:16:4, :].bitcast(I32))
        offs_sb = load_list(offs, "offs_sb")
        w1_raw = [keep.tile([P, PACK, H // 2], F32, name="w1_raw%d" % u) for u in range(2)]
        for u in range(2):
            nc.sync.dma_start(w1_raw[u][:], rows_by_partition(w1)[:, :, H // 2 * u : H // 2 * (u + 1)])
        hz_sb = load_list(hz, "hz_sb")
        table_scales = keep.tile([P, T], U8, name="table_scales")
        nc.vector.memset(table_scales[:].bitcast(I32), 0)
        for q in range(4):
            rows = slice(32 * q, 32 * q + 4)
            nc.vector.tensor_copy(table_scales[rows, :].bitcast(I32), staged_scales[rows, :].bitcast(I32))
        run_scales = keep.tile([P, T], U8, name="run_scales")
        nc.vector.memset(run_scales[:].bitcast(I32), 0)
        for r in range(2):
            nc.sync.dma_start(run_scales[r:P:16, :].bitcast(I32), x_scales[0, r:16:2, :].bitcast(I32))
        table_words = keep.tile([P, T], U32, name="table_words")
        nc.sync.dma_start(table_words[:].bitcast(I32), x_words[0].rearrange("p c r -> p (c r)").bitcast(I32))
        n1_sb = load_list(n1, "n1_sb")
        w3_raw = load_weight(w3, "w3_raw")
        gain = keep.tile([P, PACK], F32, name="gain")
        nc.sync.dma_start(gain[:], gn.rearrange("(p t) o -> p (t o)", t=PACK))
        w2_raw = load_weight(w2, "w2_raw")
        n3_sb = load_list(n3, "n3_sb")
        n2_sb = load_list(n2, "n2_sb")

        ex = [keep.tile([P, S + SPARE], F32, name="ex%d" % t) for t in range(PACK)]
        for t in range(PACK):
            nc.gpsimd.memset(ex[t][:, S:], 0.0)
        hz_scales = keep.tile([P, S], U8, name="hz_scales", align_bytes=64)
        nc.gpsimd.memset(hz_scales[:], 0)
        ident = keep.tile([P, P], F32, name="ident")
        make_identity(nc, ident[:])

        offs_scales = keep.tile([P, S], U8, name="offs_scales", align_bytes=64)
        nc.vector.tensor_copy(offs_scales[:], table_scales[:].indirect(offs_sb[:]))
        w1_dealt = keep.tile([P, PACK, P, PACK], BF16, name="w1_dealt", align_bytes=64)
        for u in range(2):
            round_and_deal(nc.scalar.copy, w1_dealt[:, :, P // 2 * u : P // 2 * (u + 1), :], w1_raw[u])
        w1_mx = quantise_dealt(w1_dealt, "w1")
        offs_words = keep.tile([P, S], U32, name="offs_words", align_bytes=64)
        nc.vector.tensor_copy(offs_words[:], table_words[:].indirect(offs_sb[:]))
        picked_run_scales = keep.tile([P, S], U8, name="picked_run_scales")
        nc.vector.tensor_copy(picked_run_scales[:], run_scales[:].indirect(hz_sb[:]))
        for r in range(4):
            nc.sync.dma_start(hz_scales[r:P:32, :].bitcast(I32), picked_run_scales[16 * (r // 2) + r % 2 : P : 32, :].bitcast(I32))

        for t in range(PACK):
            y = bank([P, S], "y%d" % t, t)
            product(y[:], w1_mx, t, (offs_words, offs_scales), slice(0, S), True, True)
            nc.scalar.activation(ex[t][:, :S], y[:], ACT.Exp, scale=0.5)

        hz_words = keep.tile([P, S], U32, name="hz_words", align_bytes=64)
        nc.vector.tensor_copy(hz_words[:], table_words[:].indirect(hz_sb[:]))
        hz_mx = (hz_words, hz_scales)

        z_codes = keep.tile([P, S], U32, name="z_codes", align_bytes=64)
        z_scales = keep.tile([P, S], U8, name="z_scales", align_bytes=64)
        z_mx = (z_codes, z_scales)
        gained = keep.tile([P, PACK, S], F32, name="gained")
        h = [keep.tile([P, S], F32, name="h%d" % t) for t in range(PACK)]
        z_rounded = keep.tile([P, S, PACK], BF16, name="z_rounded", align_bytes=64)
        h_early, sums, inverses = [], [], []

        def fetch_and_sum(b):
            width = MEMBERS * BLOCK // ENTRIES_PER_COLUMN
            entries = n1_sb[:, width * b : width * (b + 1)]
            sums.append(bank([P, PACK, P], "sums%d" % b, PACK + b))
            for t in range(PACK):
                members = keep.tile([P, MEMBERS * BLOCK], F32, name="members%d_%d" % (b, t), tag="members", bufs=BLOCKS * PACK)
                if t >= PACK - TILES_ON_VECTOR[b]:
                    nc.vector.tensor_copy(members[:], ex[t][:].indirect(entries))
                else:
                    nc.scalar.activation(members[:], ex[t][:].indirect(entries), ACT.Copy)
                for u in range(MEMBERS):
                    nc.tensor.matmul(
                        sums[b][:, t, :], lhsT=members[:, u::MEMBERS], rhs=ident[:], is_transpose=True, start=(u == 0), stop=(u == MEMBERS - 1)
                    )

        def invert(b):
            root = keep.tile([P, PACK * P], F32, name="root%d" % b)
            nc.scalar.activation(root[:], sums[b][:].rearrange("j t p -> j (t p)"), ACT.Abs_reciprocal_sqrt, scale=0.25, bias=0.125)
            turned = keep.tile([P, PACK * P], F32, name="turned%d" % b)
            nc.scalar.activation(turned[:], root[:], ACT.Square)
            inverses.append(bank([P, PACK, BLOCK], "inverse%d" % b, PACK + b))
            for t in range(PACK):
                nc.tensor.transpose(inverses[b][:, t, :], turned[:, P * t : P * (t + 1)], ident[:])

        def make_z(b):
            cols = slice(BLOCK * b, BLOCK * (b + 1))
            nc.vector.tensor_tensor(
                z_rounded[:, cols, :], inverses[b][:].rearrange("p t j -> p j t"), gained[:, :, cols].rearrange("p t j -> p j t"), ALU.mult
            )

        def quantise_z(cols):
            nc.vector.quantize_mx(
                out=z_codes[:, cols].bitcast(FP8X4), scales=z_scales[:, cols], in_=z_rounded[:, cols, :].rearrange("p j t -> p (j t)")
            )

        early, late = slice(0, S - BLOCK), slice(S - BLOCK, S)
        early_passes = (slice(0, 2 * BLOCK), slice(2 * BLOCK, 3 * BLOCK))

        w3_mx = quantise_weight(w3_raw, "w3")
        for t in range(PACK):
            h_early.append(bank([P, S - BLOCK], "h_early%d" % t, t))
            for n, cols in enumerate(early_passes):
                product(h_early[t][:, cols], w3_mx, t, hz_mx, cols, n == 0, False)

        for b in range(BLOCKS):
            fetch_and_sum(b)
        for t in range(PACK):
            nc.vector.tensor_scalar(gained[:, t, :], ex[t][:, :S], gain[:, t : t + 1], None, ALU.mult)
        w2_mx = quantise_weight(w2_raw, "w2")
        invert(0)
        for b in range(BLOCKS - 1):
            invert(b + 1)
            make_z(b)
        quantise_z(early)
        for t in range(PACK):
            for n, cols in enumerate(early_passes):
                product(h_early[t][:, cols], w2_mx, t, z_mx, cols, False, n == len(early_passes) - 1)
        make_z(BLOCKS - 1)
        quantise_z(late)
        for t in range(PACK):
            nc.scalar.copy(h[t][:, early], h_early[t][:])
        for u, move in enumerate((nc.vector.tensor_copy, nc.scalar.copy)):
            h_late = bank([P, 2, BLOCK], "h_late%d" % u, PACK + 1 + u)
            for n in range(2):
                product(h_late[:, n, :], w3_mx, 2 * u + n, hz_mx, late, n == 0, False)
            for n in range(2):
                product(h_late[:, n, :], w2_mx, 2 * u + n, z_mx, late, False, n == 1)
            for n in range(2):
                move(h[2 * u + n][:, late], h_late[:, n, :])

        out_rows = out.rearrange("(p t) j -> p t j", t=PACK)
        pieces = [(t, u) for t in range(PACK) for u in range(2)]
        for n, (t, u) in enumerate(pieces):
            entries = slice(HALF // ENTRIES_PER_COLUMN * u, HALF // ENTRIES_PER_COLUMN * (u + 1))
            at_n3 = keep.tile([P, HALF], F32, name="at_n3_%d" % n)
            nc.scalar.activation(at_n3[:], h[t][:].indirect(n3_sb[:, entries]), ACT.Copy)
            gap = keep.tile([P, HALF], F32, name="gap%d" % n)
            at_n2 = h[t][:].indirect(n2_sb[:, entries])
            if n == 0:
                fetched = keep.tile([P, HALF], F32, name="at_n2_%d" % n)
                nc.vector.tensor_copy(fetched[:], at_n2)
                at_n2 = fetched[:]
            elif n >= len(pieces) - BOTH_ON_SCALAR:
                fetched = keep.tile([P, HALF], F32, name="at_n2_%d" % n)
                nc.scalar.activation(fetched[:], at_n2, ACT.Copy)
                at_n2 = fetched[:]
            nc.vector.tensor_tensor(gap[:], at_n2, at_n3[:], ALU.subtract)
            nc.sync.dma_start(out_rows[:, t, HALF * u : HALF * (u + 1)], gap[:])
